import numpy as np
CORES = [93,349,221,477]
N = 4
ROOT = 3
def setup_inputs(rng):
    return {"x": rng.standard_normal((N, 128, N * 256), dtype=np.float32)}
def reference(x):
    return {"y": np.stack([x[ROOT][:, r * 256:(r + 1) * 256] for r in range(N)])}

@@ -1,0 +1,61 @@
+from concourse.bass import DstId, RemoteDMATransfer
+
+SCRATCH = {
+    "h": ("dram", [2, 128, 128], "float32"),
+    "b0": ("dram", [128, 256], "float32"),
+    "b1": ("dram", [128, 256], "float32"),
+}
+SEMAPHORES = ["ld2", "ld01", "own", "sent", "arr", "arrb", "st", "stb"]
+
+W = 256
+LO, HI = 0x0F, 0xF0
+
+
+def rank_program(g, core, T, topo):
+    c0, c1, c2, root = T.cores
+    relay_a = c1 - 1
+    relay_b = c0 - 1
+    s = T.sem
+
+    def dst(d):
+        rid, pid = topo.addr(d, core)
+        return DstId(rid=rid, pnc=pid)
+
+    if core == root:
+        g.sync.dma_start(T.h[0], T.x[0:64, 2 * W:3 * W]).then_inc(s.ld2, 16)
+        g.scalar.dma_start(T.h[1], T.x[64:128, 2 * W:3 * W]).then_inc(s.ld2, 16)
+        g.sync.dma_start(T.b1[:], T.x[:, W:2 * W]).then_inc(s.ld01, 16)
+        g.scalar.dma_start(T.b0[:], T.x[:, 0:W]).then_inc(s.ld01, 16)
+        g.sync.dma_start(T.y[0:64, :], T.x[0:64, 3 * W:4 * W]).then_inc(s.own, 16)
+        g.scalar.dma_start(T.y[64:128, :], T.x[64:128, 3 * W:4 * W]).then_inc(s.own, 16)
+
+        g.wait_ge(s.ld2, 32)
+        g.remote_dma_fused([
+            RemoteDMATransfer(dst_ids=[dst(relay_a)], dma_engine_mask=LO, remote_sem=s.arr, src=T.h[0], dst=T.h[0]),
+            RemoteDMATransfer(dst_ids=[dst(relay_b)], dma_engine_mask=HI, remote_sem=s.arr, src=T.h[1], dst=T.h[1]),
+        ], local_sem=s.sent)
+        g.wait_ge(s.ld01, 32)
+        g.remote_dma_fused([
+            RemoteDMATransfer(dst_ids=[dst(c1)], dma_engine_mask=LO, remote_sem=s.arr, src=T.b1[:], dst=T.b1[:]),
+            RemoteDMATransfer(dst_ids=[dst(c0)], dma_engine_mask=HI, remote_sem=s.arr, src=T.b0[:], dst=T.b0[:]),
+        ], local_sem=s.sent)
+        g.wait_ge(s.sent, 16)
+        g.wait_ge(s.own, 32)
+    elif core == relay_a or core == relay_b:
+        k = 0 if core == relay_a else 1
+        rid, pid = topo.addr(c2, core)
+        g.wait_ge(s.arr, 4)
+        g.remote_dma(T.h[k], T.h[k], s.arr if k == 0 else s.arrb, s.sent, pid, rid, 0xFF)
+        g.wait_ge(s.sent, 8)
+    elif core == c0 or core == c1:
+        land = T.b0 if core == c0 else T.b1
+        g.sync.wait_ge(s.arr, 4)
+        g.sync.dma_start(T.y[:, :], land[:]).then_inc(s.st, 16)
+        g.sync.wait_ge(s.st, 16)
+    elif core == c2:
+        g.sync.wait_ge(s.arr, 8)
+        g.sync.dma_start(T.y[0:64, :], T.h[0]).then_inc(s.st, 16)
+        g.scalar.wait_ge(s.arrb, 8)
+        g.scalar.dma_start(T.y[64:128, :], T.h[1]).then_inc(s.stb, 16)
+        g.sync.wait_ge(s.st, 16)
+        g.scalar.wait_ge(s.stb, 16)

@@ -1,20 +1,19 @@
 from concourse.bass import DstId, RemoteDMATransfer
 
 SCRATCH = {
-    "h": ("dram", [2, 128, 128], "float32"),
-    "b0": ("dram", [128, 256], "float32"),
+    "q2": ("dram", [4, 128, 64], "float32"),
+    "q0": ("dram", [4, 128, 64], "float32"),
     "b1": ("dram", [128, 256], "float32"),
 }
-SEMAPHORES = ["ld2", "ld01", "own", "sent", "arr", "arrb", "st", "stb"]
+SEMAPHORES = ["ld", "ld1", "own", "sent", "arr", "st"]
 
 W = 256
-LO, HI = 0x0F, 0xF0
 
 
 def rank_program(g, core, T, topo):
     c0, c1, c2, root = T.cores
-    relay_a = c1 - 1
-    relay_b = c0 - 1
+    helpers = [root - root % 8 + 2 * q for q in range(4)]
+    relays = [c1 - c1 % 8 + 2 * q for q in range(4)]
     s = T.sem
 
     def dst(d):
@@ -22,40 +21,38 @@ def rank_program(g, core, T, topo):
         return DstId(rid=rid, pnc=pid)
 
     if core == root:
-        g.sync.dma_start(T.h[0], T.x[0:64, 2 * W:3 * W]).then_inc(s.ld2, 16)
-        g.scalar.dma_start(T.h[1], T.x[64:128, 2 * W:3 * W]).then_inc(s.ld2, 16)
-        g.sync.dma_start(T.b1[:], T.x[:, W:2 * W]).then_inc(s.ld01, 16)
-        g.scalar.dma_start(T.b0[:], T.x[:, 0:W]).then_inc(s.ld01, 16)
-        g.sync.dma_start(T.y[0:64, :], T.x[0:64, 3 * W:4 * W]).then_inc(s.own, 16)
-        g.scalar.dma_start(T.y[64:128, :], T.x[64:128, 3 * W:4 * W]).then_inc(s.own, 16)
+        g.sync.dma_start(T.q2[:], T.x[:, 2 * W:3 * W]).then_inc(s.ld, 16)
+        g.scalar.dma_start(T.q0[:], T.x[:, 0:W]).then_inc(s.ld, 16)
+        g.sync.dma_start(T.b1[:], T.x[:, W:2 * W]).then_inc(s.ld1, 16)
+        g.scalar.dma_start(T.y[:, :], T.x[:, 3 * W:4 * W]).then_inc(s.own, 16)
 
-        g.wait_ge(s.ld2, 32)
-        g.remote_dma_fused([
-            RemoteDMATransfer(dst_ids=[dst(relay_a)], dma_engine_mask=LO, remote_sem=s.arr, src=T.h[0], dst=T.h[0]),
-            RemoteDMATransfer(dst_ids=[dst(relay_b)], dma_engine_mask=HI, remote_sem=s.arr, src=T.h[1], dst=T.h[1]),
-        ], local_sem=s.sent)
-        g.wait_ge(s.ld01, 32)
-        g.remote_dma_fused([
-            RemoteDMATransfer(dst_ids=[dst(c1)], dma_engine_mask=LO, remote_sem=s.arr, src=T.b1[:], dst=T.b1[:]),
-            RemoteDMATransfer(dst_ids=[dst(c0)], dma_engine_mask=HI, remote_sem=s.arr, src=T.b0[:], dst=T.b0[:]),
-        ], local_sem=s.sent)
-        g.wait_ge(s.sent, 16)
-        g.wait_ge(s.own, 32)
-    elif core == relay_a or core == relay_b:
-        k = 0 if core == relay_a else 1
-        rid, pid = topo.addr(c2, core)
-        g.wait_ge(s.arr, 4)
-        g.remote_dma(T.h[k], T.h[k], s.arr if k == 0 else s.arrb, s.sent, pid, rid, 0xFF)
+        g.wait_ge(s.ld, 32)
+        g.remote_dma_fused(
+            [RemoteDMATransfer(dst_ids=[dst(relays[q])], dma_engine_mask=0x3 << (2 * q), remote_sem=s.arr,
+                               src=T.q2[q], dst=T.q2[q]) for q in range(4)]
+            + [RemoteDMATransfer(dst_ids=[dst(helpers[q])], dma_engine_mask=0x300 << (2 * q), remote_sem=s.arr,
+                                 src=T.q0[q], dst=T.q0[q]) for q in range(4)],
+            local_sem=s.sent)
+        g.wait_ge(s.ld1, 16)
+        rid, pid = topo.addr(c1, core)
+        g.remote_dma(T.b1[:], T.b1[:], s.arr, s.sent, pid, rid, 0xFF)
+        g.wait_ge(s.sent, 24)
+        g.wait_ge(s.own, 16)
+    elif core in helpers or core in relays:
+        if core in helpers:
+            q, buf, to = helpers.index(core), T.q0, c0
+        else:
+            q, buf, to = relays.index(core), T.q2, c2
+        rid, pid = topo.addr(to, core)
+        g.wait_ge(s.arr, 2)
+        g.remote_dma(buf[q], buf[q], s.arr, s.sent, pid, rid, 0xFF)
         g.wait_ge(s.sent, 8)
-    elif core == c0 or core == c1:
-        land = T.b0 if core == c0 else T.b1
-        g.sync.wait_ge(s.arr, 4)
+    elif core == c0 or core == c2:
+        land = T.q0 if core == c0 else T.q2
+        g.sync.wait_ge(s.arr, 32)
         g.sync.dma_start(T.y[:, :], land[:]).then_inc(s.st, 16)
         g.sync.wait_ge(s.st, 16)
-    elif core == c2:
+    elif core == c1:
         g.sync.wait_ge(s.arr, 8)
-        g.sync.dma_start(T.y[0:64, :], T.h[0]).then_inc(s.st, 16)
-        g.scalar.wait_ge(s.arrb, 8)
-        g.scalar.dma_start(T.y[64:128, :], T.h[1]).then_inc(s.stb, 16)
+        g.sync.dma_start(T.y[:, :], T.b1[:]).then_inc(s.st, 16)
         g.sync.wait_ge(s.st, 16)
-        g.scalar.wait_ge(s.stb, 16)

@@ -1,11 +1,15 @@
 from concourse.bass import DstId, RemoteDMATransfer
 
+NW = 2
+RW = 128 // NW
+PC = 256 // (4 * NW)
+
 SCRATCH = {
-    "q2": ("dram", [4, 128, 64], "float32"),
-    "q0": ("dram", [4, 128, 64], "float32"),
+    "q2": ("dram", [4 * NW, 128, PC], "float32"),
+    "q0": ("dram", [4 * NW, 128, PC], "float32"),
     "b1": ("dram", [128, 256], "float32"),
 }
-SEMAPHORES = ["ld", "ld1", "own", "sent", "arr", "st"]
+SEMAPHORES = ["ldb", "own", "sent", "ld0", "ld1", "arr0", "arr1", "st0", "st1"]
 
 W = 256
 
@@ -21,22 +25,26 @@ def rank_program(g, core, T, topo):
         return DstId(rid=rid, pnc=pid)
 
     if core == root:
-        g.sync.dma_start(T.q2[:], T.x[:, 2 * W:3 * W]).then_inc(s.ld, 16)
-        g.scalar.dma_start(T.q0[:], T.x[:, 0:W]).then_inc(s.ld, 16)
-        g.sync.dma_start(T.b1[:], T.x[:, W:2 * W]).then_inc(s.ld1, 16)
+        for e in range(NW):
+            r = slice(e * RW, (e + 1) * RW)
+            k = slice(4 * e, 4 * e + 4)
+            g.sync.dma_start(T.q2[k], T.x[r, 2 * W:3 * W]).then_inc(s["ld%d" % e], 16)
+            g.scalar.dma_start(T.q0[k], T.x[r, 0:W]).then_inc(s["ld%d" % e], 16)
+        g.sync.dma_start(T.b1[:], T.x[:, W:2 * W]).then_inc(s.ldb, 16)
         g.scalar.dma_start(T.y[:, :], T.x[:, 3 * W:4 * W]).then_inc(s.own, 16)
 
-        g.wait_ge(s.ld, 32)
-        g.remote_dma_fused(
-            [RemoteDMATransfer(dst_ids=[dst(relays[q])], dma_engine_mask=0x3 << (2 * q), remote_sem=s.arr,
-                               src=T.q2[q], dst=T.q2[q]) for q in range(4)]
-            + [RemoteDMATransfer(dst_ids=[dst(helpers[q])], dma_engine_mask=0x300 << (2 * q), remote_sem=s.arr,
-                                 src=T.q0[q], dst=T.q0[q]) for q in range(4)],
-            local_sem=s.sent)
-        g.wait_ge(s.ld1, 16)
+        for e in range(NW):
+            g.wait_ge(s["ld%d" % e], 32)
+            g.remote_dma_fused(
+                [RemoteDMATransfer(dst_ids=[dst(relays[q])], dma_engine_mask=0x3 << (2 * q), remote_sem=s["arr%d" % e],
+                                   src=T.q2[4 * e + q], dst=T.q2[4 * e + q]) for q in range(4)]
+                + [RemoteDMATransfer(dst_ids=[dst(helpers[q])], dma_engine_mask=0x300 << (2 * q), remote_sem=s["arr%d" % e],
+                                     src=T.q0[4 * e + q], dst=T.q0[4 * e + q]) for q in range(4)],
+                local_sem=s.sent)
+        g.wait_ge(s.ldb, 16)
         rid, pid = topo.addr(c1, core)
-        g.remote_dma(T.b1[:], T.b1[:], s.arr, s.sent, pid, rid, 0xFF)
-        g.wait_ge(s.sent, 24)
+        g.remote_dma(T.b1[:], T.b1[:], s.arr0, s.sent, pid, rid, 0xFF)
+        g.wait_ge(s.sent, 16 * NW + 8)
         g.wait_ge(s.own, 16)
     elif core in helpers or core in relays:
         if core in helpers:
@@ -44,15 +52,20 @@ def rank_program(g, core, T, topo):
         else:
             q, buf, to = relays.index(core), T.q2, c2
         rid, pid = topo.addr(to, core)
-        g.wait_ge(s.arr, 2)
-        g.remote_dma(buf[q], buf[q], s.arr, s.sent, pid, rid, 0xFF)
-        g.wait_ge(s.sent, 8)
+        for e in range(NW):
+            g.wait_ge(s["arr%d" % e], 2)
+            g.remote_dma(buf[4 * e + q], buf[4 * e + q], s["arr%d" % e], s.sent, pid, rid, 0x0F << (4 * (e % 2)))
+        g.wait_ge(s.sent, 4 * NW)
     elif core == c0 or core == c2:
         land = T.q0 if core == c0 else T.q2
-        g.sync.wait_ge(s.arr, 32)
-        g.sync.dma_start(T.y[:, :], land[:]).then_inc(s.st, 16)
-        g.sync.wait_ge(s.st, 16)
+        for e in range(NW):
+            qu = g.scalar if e % 2 == 0 else g.sync
+            qu.wait_ge(s["arr%d" % e], 16)
+            qu.dma_start(T.y[e * RW:(e + 1) * RW, :], land[4 * e:4 * e + 4]).then_inc(s["st%d" % e], 16)
+        for e in range(NW):
+            qu = g.scalar if e % 2 == 0 else g.sync
+            qu.wait_ge(s["st%d" % e], 16)
     elif core == c1:
-        g.sync.wait_ge(s.arr, 8)
-        g.sync.dma_start(T.y[:, :], T.b1[:]).then_inc(s.st, 16)
-        g.sync.wait_ge(s.st, 16)
+        g.sync.wait_ge(s.arr0, 8)
+        g.sync.dma_start(T.y[:, :], T.b1[:]).then_inc(s.st0, 16)
+        g.sync.wait_ge(s.st0, 16)

from concourse.bass import DstId, RemoteDMATransfer

NW = 2
RW = 128 // NW
PC = 256 // (4 * NW)

SCRATCH = {
    "q2": ("dram", [4 * NW, 128, PC], "float32"),
    "q0": ("dram", [4 * NW, 128, PC], "float32"),
    "b1": ("dram", [128, 256], "float32"),
}
SEMAPHORES = ["ldb", "own", "sent", "ld0", "ld1", "arr0", "arr1", "st0", "st1"]

W = 256


def rank_program(g, core, T, topo):
    c0, c1, c2, root = T.cores
    helpers = [root - root % 8 + 2 * q for q in range(4)]
    relays = [c1 - c1 % 8 + 2 * q for q in range(4)]
    s = T.sem

    def dst(d):
        rid, pid = topo.addr(d, core)
        return DstId(rid=rid, pnc=pid)

    if core == root:
        for e in range(NW):
            r = slice(e * RW, (e + 1) * RW)
            k = slice(4 * e, 4 * e + 4)
            g.sync.dma_start(T.q2[k], T.x[r, 2 * W:3 * W]).then_inc(s["ld%d" % e], 16)
            g.scalar.dma_start(T.q0[k], T.x[r, 0:W]).then_inc(s["ld%d" % e], 16)
        g.sync.dma_start(T.b1[:], T.x[:, W:2 * W]).then_inc(s.ldb, 16)
        g.scalar.dma_start(T.y[:, :], T.x[:, 3 * W:4 * W]).then_inc(s.own, 16)

        for e in range(NW):
            g.wait_ge(s["ld%d" % e], 32)
            g.remote_dma_fused(
                [RemoteDMATransfer(dst_ids=[dst(relays[q])], dma_engine_mask=0x3 << (2 * q), remote_sem=s["arr%d" % e],
                                   src=T.q2[4 * e + q], dst=T.q2[4 * e + q]) for q in range(4)]
                + [RemoteDMATransfer(dst_ids=[dst(helpers[q])], dma_engine_mask=0x300 << (2 * q), remote_sem=s["arr%d" % e],
                                     src=T.q0[4 * e + q], dst=T.q0[4 * e + q]) for q in range(4)],
                local_sem=s.sent)
        g.wait_ge(s.ldb, 16)
        rid, pid = topo.addr(c1, core)
        g.remote_dma(T.b1[:], T.b1[:], s.arr0, s.sent, pid, rid, 0xFF)
        g.wait_ge(s.sent, 16 * NW + 8)
        g.wait_ge(s.own, 16)
    elif core in helpers or core in relays:
        if core in helpers:
            q, buf, to = helpers.index(core), T.q0, c0
        else:
            q, buf, to = relays.index(core), T.q2, c2
        rid, pid = topo.addr(to, core)
        for e in range(NW):
            g.wait_ge(s["arr%d" % e], 2)
            g.remote_dma(buf[4 * e + q], buf[4 * e + q], s["arr%d" % e], s.sent, pid, rid, 0x0F << (4 * (e % 2)))
        g.wait_ge(s.sent, 4 * NW)
    elif core == c0 or core == c2:
        land = T.q0 if core == c0 else T.q2
        for e in range(NW):
            qu = g.scalar if e % 2 == 0 else g.sync
            qu.wait_ge(s["arr%d" % e], 16)
            qu.dma_start(T.y[e * RW:(e + 1) * RW, :], land[4 * e:4 * e + 4]).then_inc(s["st%d" % e], 16)
        for e in range(NW):
            qu = g.scalar if e % 2 == 0 else g.sync
            qu.wait_ge(s["st%d" % e], 16)
    elif core == c1:
        g.sync.wait_ge(s.arr0, 8)
        g.sync.dma_start(T.y[:, :], T.b1[:]).then_inc(s.st0, 16)
        g.sync.wait_ge(s.st0, 16)
